import numpy as np
import ml_dtypes


def mxq(x, axis, fmt="e4m3"):
    dtype, down = {"e4m3": (ml_dtypes.float8_e4m3fn, 7), "e5m2": (ml_dtypes.float8_e5m2, 14)}[fmt]
    v = np.moveaxis(np.asarray(x, np.float32).astype(ml_dtypes.bfloat16).astype(np.float64), axis, -1)
    blocks = v.reshape(v.shape[:-1] + (-1, 32))
    amax = np.abs(blocks).max(-1, keepdims=True)
    byte = np.maximum(np.where(amax > 0, np.frexp(amax)[1] - 1 + 127, 0) - down, 1)
    scale = np.exp2(byte - 127.0)
    codes = (blocks / scale).astype(np.float32).astype(dtype).astype(np.float64)
    return np.moveaxis((codes * scale).reshape(v.shape), -1, axis)


WIDE = False


def mx_kscale(k):
    if not WIDE:
        return np.ones(k)
    levels = np.array([10, -10, 5, -5, 0])
    if k % 512:
        return np.exp2(np.random.permutation(np.resize(levels, k // 32))).repeat(32)
    a = np.empty((k // 512, 16))
    for p in range(k // 512):
        a[p, :8] = np.random.permutation(np.resize(levels, 8))
        for g in range(8):
            far = levels[np.abs(levels - a[p, g]) >= 10]
            a[p, g + 8] = far[np.random.randint(len(far))]
    return np.exp2(a.ravel()).repeat(32)


def f64(x):
    return np.asarray(x).astype(np.float64)


def striped(idx):
    return np.tile(idx.reshape(-1, 16).T, (8, 1)).astype(np.uint16)


def unstriped(offs):
    return offs[:16].T.reshape(-1).astype(np.int64)


def pack_weight(w):
    k, n = w.shape
    w = f64(np.asarray(w, np.float32).astype(ml_dtypes.bfloat16)).reshape(k // 32, 32, n)
    amax = np.abs(w).max(1)
    byte = np.clip(np.where(amax > 0, np.frexp(amax)[1] - 1 + 127 - 7, 1), 1, 254)
    scaled = (w * np.exp2(127.0 - byte)[:, None, :]).reshape(k, n).astype(np.float32)
    words = np.ascontiguousarray(scaled.reshape(k // 512, 128, 4, n).transpose(0, 1, 3, 2)).astype(ml_dtypes.float8_e4m3fn).view(np.uint8)
    return words, np.ascontiguousarray(byte.astype(np.uint8).reshape(k // 512, 16, n))


def unpack_weight(words, scales):
    g, p, n, _ = words.shape
    vals = np.ascontiguousarray(words).view(ml_dtypes.float8_e4m3fn).astype(np.float64) * np.repeat(np.exp2(scales.astype(np.float64) - 127.0), 8, axis=1)[..., None]
    return vals.transpose(0, 1, 3, 2).reshape(g * 512, n)


E2M1 = np.array([0.0, 0.5, 1.0, 1.5, 2.0, 3.0, 4.0, 6.0, -0.0, -0.5, -1.0, -1.5, -2.0, -3.0, -4.0, -6.0])


def pack_fp4(w):
    k, n = w.shape
    w = f64(np.asarray(w, np.float32).astype(ml_dtypes.bfloat16)).reshape(k // 32, 32, n)
    amax = np.abs(w).max(1)
    mant, ex = np.frexp(amax / 6.0)
    byte = np.clip(np.where(amax > 0, np.where(mant > 0.5, ex, ex - 1) + 127, 1), 1, 254)
    scaled = (w * np.exp2(127.0 - byte)[:, None, :]).reshape(k, n).astype(np.float32)
    c = np.ascontiguousarray(scaled.reshape(k // 512, 128, 4, n).transpose(0, 1, 3, 2)).astype(ml_dtypes.float4_e2m1fn).view(np.uint8) & 0xF
    words = (c[..., 0::2] | (c[..., 1::2] << 4)).reshape(k // 512, 128, 2 * n)
    return np.ascontiguousarray(words), np.ascontiguousarray(byte.astype(np.uint8).reshape(k // 512, 16, n))


def unpack_fp4(words, scales):
    g, _, n = scales.shape
    words = np.ascontiguousarray(words).reshape(g, 128, n, 2)
    nib = np.empty((g, 128, n, 4), np.uint8)
    nib[..., 0::2] = words & 0xF
    nib[..., 1::2] = words >> 4
    vals = E2M1[nib] * np.repeat(np.exp2(scales.astype(np.float64) - 127.0), 8, axis=1)[..., None]
    return vals.transpose(0, 1, 3, 2).reshape(g * 512, n)


def sigmoid(v):
    return 1.0 / (1.0 + np.exp(-np.maximum(v, -700.0)))

def planes(y):
    n, m = y.shape
    v = y.astype(np.float32).astype(ml_dtypes.bfloat16).astype(np.float64).reshape(n // 32, 32, m)
    top = np.abs(v).max(1)
    byte = np.clip(np.where(top > 0, np.frexp(top)[1] - 1 + 127 - 7, 1), 1, 254)
    codes = (v * np.exp2(127.0 - byte)[:, None, :]).reshape(n, m).astype(np.float32).astype(ml_dtypes.float8_e4m3fn).view(np.uint8)
    words = codes.reshape(n // 512, 128, 4, m).transpose(0, 1, 3, 2)
    return np.ascontiguousarray(words), np.ascontiguousarray(byte.astype(np.uint8).reshape(n // 512, 16, m))


K, T, S, H, C = 512, 2048, 256, 512, 512


def setup_inputs():
    n = np.random.standard_normal
    s = mx_kscale(K)[:, None]
    packed_xT = pack_weight(n((K, T)) * s)
    packed_w1 = pack_fp4(n((K, H)) / np.sqrt(K) / s)
    packed_w2 = pack_fp4(n((K, H)) / np.sqrt(K) / s)
    return {
        "x_words": packed_xT[0],
        "x_scales": packed_xT[1],
        "w1_words": packed_w1[0],
        "w1_scales": packed_w1[1],
        "w2_words": packed_w2[0],
        "w2_scales": packed_w2[1],
        "sl": np.random.uniform(1.0, 2.0, (H, 1)).astype(np.float32),
        "th": (0.5 * n((H, 1))).astype(np.float32),
        "gs": (np.random.uniform(0.5, 1.5, (K, 1)) / s).astype(np.float32),
        "sl2": np.random.uniform(1.0, 2.0, (C, 1)).astype(np.float32),
        "offs": striped(np.random.permutation(T)[:S]),
        "two": striped(np.random.permutation(T)[:S]),
        "n1": striped(np.random.permutation(S)),
        "n2": striped(np.random.permutation(S)),
        "cand": striped(np.random.permutation(T)[:C]),
        "n3": striped(np.random.permutation(S)),
    }


def reference(x_words, x_scales, w1_words, w1_scales, w2_words, w2_scales, sl, th, gs, sl2, offs, two, n1, n2, cand, n3):
    x_cand = unpack_weight(x_words, x_scales)[:, unstriped(cand)]
    xq = unpack_weight(x_words, x_scales)[:, unstriped(offs)]
    y = unpack_fp4(w1_words, w1_scales).T @ xq
    x_two = unpack_weight(x_words, x_scales)[:, unstriped(two)]
    d = unpack_fp4(w2_words, w2_scales).T @ x_two
    sg = sigmoid(f64(sl) * (d[:, unstriped(n1)] - f64(th)))
    z = f64(gs) * (np.maximum(y * sg, d[:, unstriped(n2)] - d))
    s = 0.0625 * ((x_cand.T @ mxq(z, 0, "e4m3")))
    mu = s.mean(axis=1, keepdims=True)
    sg2 = sigmoid(f64(sl2) * (s[:, unstriped(n3)] - mu))
    out_0 = (s - mu) * sg2
    return (out_0,) + planes(out_0)

@@ -1,0 +1,187 @@
+from contextlib import ExitStack
+
+import concourse.mybir as mybir
+
+K, T, S, H, C = 512, 2048, 256, 512, 512
+FLOPS = 2 * K * S * (H + H + C)
+
+F32 = mybir.dt.float32
+BF16 = mybir.dt.bfloat16
+I32 = mybir.dt.int32
+U32 = mybir.dt.uint32
+U16 = mybir.dt.uint16
+U8 = mybir.dt.uint8
+FP8X4 = mybir.dt.float8_e4m3fn_x4
+FP4X4 = mybir.dt.float4_e2m1fn_x4
+ALU = mybir.AluOpType
+ACT = mybir.ActivationFunctionType
+
+P = 128
+PACK = 4
+WINDOW = 2 * S
+
+
+def tile_picked_twcmxbecn_none_po_kernel(tc, x_words, x_scales, w1_words, w1_scales, w2_words, w2_scales, sl, th, gs, sl2, offs, two, n1, n2, cand, n3, out_0, out_1, out_2):
+    nc = tc.nc
+    with ExitStack() as ctx:
+        keep = ctx.enter_context(tc.tile_pool(name="keep", bufs=1))
+        psum = ctx.enter_context(tc.psum_pool(name="psum", bufs=1))
+
+        def sb(name, shape, dtype, tag=""):
+            return keep.tile(shape, dtype, name=name, tag=tag or name, align_bytes=64)
+
+        def load_list(name, src):
+            tile = sb(name, list(src.shape), U16)
+            nc.sync.dma_start(tile[:], src)
+            return tile
+
+        def load_plane(queue, tile, src):
+            words = src.shape[2] // 4
+            for q in range(4):
+                queue.dma_start(tile[32 * q : 32 * q + 32, :].bitcast(I32), src[0, 4 * q : 4 * q + 4, :].bitcast(I32).unsqueeze(0).to_broadcast([8, 4, words]))
+
+        def load_rows(queue, name, src):
+            tile = sb(name, [P, PACK], F32)
+            queue.dma_start(tile[:], src.rearrange("(p t) o -> p (t o)", t=PACK))
+            return tile
+
+        xs = sb("xs", [P, T], U8)
+        load_plane(nc.sync, xs, x_scales)
+        two_sb = load_list("two_sb", two)
+        offs_sb = load_list("offs_sb", offs)
+        cand_sb = load_list("cand_sb", cand)
+        xw = sb("xw", [P, T], U32)
+        nc.sync.dma_start(xw[:].bitcast(I32), x_words[0].rearrange("p n t -> p (n t)").bitcast(I32))
+        w2w_raw = sb("w2w_raw", [P, 2 * H], U8)
+        w1w_raw = sb("w1w_raw", [P, 2 * H], U8)
+        w2s_raw = sb("w2s_raw", [P, H], U8)
+        w1s_raw = sb("w1s_raw", [P, H], U8)
+        nc.sync.dma_start(w2w_raw[:].bitcast(I32), w2_words[0].bitcast(I32))
+        load_plane(nc.sync, w2s_raw, w2_scales)
+        n1_sb = load_list("n1_sb", n1)
+        n2_sb = load_list("n2_sb", n2)
+        nc.sync.dma_start(w1w_raw[:].bitcast(I32), w1_words[0].bitcast(I32))
+        load_plane(nc.sync, w1s_raw, w1_scales)
+        n3_sb = load_list("n3_sb", n3)
+        sl_sb = load_rows(nc.gpsimd, "sl_sb", sl)
+        th_sb = load_rows(nc.gpsimd, "th_sb", th)
+        gs_sb = load_rows(nc.gpsimd, "gs_sb", gs)
+        sl2_sb = load_rows(nc.gpsimd, "sl2_sb", sl2)
+
+        def gather(name, table, offsets, n, dtype, tag=""):
+            tile = sb(name, [P, n], dtype, tag)
+            nc.vector.tensor_copy(tile[:], table[:].indirect(offsets[:]))
+            return tile
+
+        def gather_dealt(name, table, offsets, n, dtype, tag=""):
+            tile = sb(name, [P, n], dtype, tag)
+            nc.vector.tensor_copy(tile[:].rearrange("p (t m) -> p m t", t=PACK), table[:].indirect(offsets[:]))
+            return tile
+
+        def deal_words(name, raw):
+            tile = sb(name, [P, 2 * H], U8)
+            nc.scalar.copy(tile[:].bitcast(U16).rearrange("p (t m) -> p t m", t=PACK), raw[:].bitcast(U16).rearrange("p (m t) -> p t m", t=PACK))
+            return tile
+
+        def deal_bytes(name, raw):
+            tile = sb(name, [P, H], U8)
+            nc.vector.tensor_copy(tile[:].rearrange("p (t m) -> p t m", t=PACK), raw[:].rearrange("p (m t) -> p t m", t=PACK))
+            return tile
+
+        two_s = gather("two_s", xs, two_sb, S, U8)
+        offs_s = gather("offs_s", xs, offs_sb, S, U8)
+        cand_s = gather_dealt("cand_s", xs, cand_sb, C, U8)
+        w2w = deal_words("w2w", w2w_raw)
+        two_w = gather("two_w", xw, two_sb, S, U32)
+        w2s = deal_bytes("w2s", w2s_raw)
+        w1w = deal_words("w1w", w1w_raw)
+        offs_w = gather("offs_w", xw, offs_sb, S, U32, "w2s_raw")
+
+        nb = sb("nb", [P, PACK], F32)
+        slth = sb("slth", [P, PACK], F32)
+        nc.gpsimd.tensor_tensor(slth[:], sl_sb[:], th_sb[:], ALU.mult)
+        nc.gpsimd.tensor_scalar(nb[:], slth[:], -1.0, 0.0, ALU.mult, ALU.add)
+
+        def weight_product(bank, words, scales, t, xw_g, xs_g):
+            nc.tensor.matmul_mx(
+                out=bank[:],
+                lhsT=words[:, 2 * P * t : 2 * P * (t + 1)].bitcast(FP4X4),
+                lhsT_scale=scales[:, P * t : P * (t + 1)],
+                rhs=xw_g[:].bitcast(FP8X4),
+                rhs_scale=xs_g[:],
+                start=True,
+                stop=True,
+            )
+
+        d_ps = [psum.tile([P, S], F32, name=f"d_ps{t}", tag=f"first{t}") for t in range(PACK)]
+        y_ps = [psum.tile([P, S], F32, name=f"y_ps{t}") for t in range(PACK)]
+        for t in range(PACK):
+            weight_product(d_ps[t], w2w, w2s, t, two_w, two_s)
+        w1s = deal_bytes("w1s", w1s_raw)
+        for t in range(PACK):
+            weight_product(y_ps[t], w1w, w1s, t, offs_w, offs_s)
+
+        cand_w = gather_dealt("cand_w", xw, cand_sb, C, U32, "w1s_raw")
+
+        d_win = [sb(f"d_win{t}", [P, WINDOW], F32) for t in range(PACK)]
+        sg = sb("sg", [P, PACK, S], F32)
+        dn2 = sb("dn2", [P, PACK, S], F32)
+        ysg = sb("ysg", [P, PACK, S], F32)
+        diff = sb("diff", [P, PACK, S], F32)
+        larger = sb("larger", [P, PACK, S], F32)
+        for t in range(PACK):
+            nc.scalar.copy(d_win[t][:, :S], d_ps[t][:])
+            nc.scalar.activation(sg[:, t, :], d_win[t][:].indirect(n1_sb[:]), ACT.Sigmoid, bias=nb[:, t : t + 1], scale=sl_sb[:, t : t + 1])
+            nc.scalar.activation(dn2[:, t, :], d_win[t][:].indirect(n2_sb[:]), ACT.Copy)
+            nc.vector.tensor_tensor(ysg[:, t, :], y_ps[t][:], sg[:, t, :], ALU.mult)
+            nc.vector.tensor_tensor(diff[:, t, :], dn2[:, t, :], d_win[t][:, :S], ALU.subtract)
+            nc.vector.tensor_tensor(larger[:, t, :], ysg[:, t, :], diff[:, t, :], ALU.max)
+
+        z_bf = sb("z_bf", [P, S, PACK], BF16)
+        nc.vector.tensor_tensor(
+            z_bf[:].rearrange("p (c i) t -> p c t i", i=4),
+            larger[:].rearrange("p t (c i) -> p c t i", i=4),
+            gs_sb[:].unsqueeze(1).unsqueeze(3).to_broadcast([P, S // 4, PACK, 4]),
+            ALU.mult,
+        )
+        z_w = sb("z_w", [P, S], U32)
+        z_s = sb("z_s", [P, S], U8)
+        nc.vector.quantize_mx(out=z_w[:].bitcast(FP8X4), scales=z_s[:], in_=z_bf[:].rearrange("p j t -> p (j t)"))
+
+        coef = sb("coef", [P, 2, PACK], F32)
+        nc.gpsimd.memset(coef[:, 0, :], 1.0 / S)
+        nc.gpsimd.tensor_scalar(coef[:, 1, :], sl2_sb[:], -1.0 / S, 0.0, ALU.mult, ALU.add)
+
+        s_win = [sb(f"s_win{t}", [P, WINDOW], F32) for t in range(PACK)]
+        total = sb("total", [P, PACK], F32)
+        stat = sb("stat", [P, PACK, 2], F32)
+        sg2 = sb("sg2", [P, PACK, S], F32)
+        res = sb("res", [P, PACK, S], F32)
+        out_rows = out_0.rearrange("(p t) j -> p t j", t=PACK)
+        for t in range(PACK):
+            s_ps = psum.tile([P, S], F32, name=f"s_ps{t}", tag=f"first{t}")
+            nc.tensor.matmul_mx(
+                out=s_ps[:],
+                lhsT=cand_w[:, P * t : P * (t + 1)].bitcast(FP8X4),
+                lhsT_scale=cand_s[:, P * t : P * (t + 1)],
+                rhs=z_w[:].bitcast(FP8X4),
+                rhs_scale=z_s[:],
+                start=True,
+                stop=True,
+            )
+            nc.vector.tensor_scalar(s_win[t][:, :S], s_ps[:], 0.0625, None, ALU.mult, ALU.add, accum_out=total[:, t : t + 1])
+            nc.vector.tensor_scalar(stat[:, t, :], coef[:, :, t], total[:, t : t + 1], None, ALU.mult)
+        for t in range(PACK):
+            nc.scalar.activation(sg2[:, t, :], s_win[t][:].indirect(n3_sb[:]), ACT.Sigmoid, bias=stat[:, t, 1:2], scale=sl2_sb[:, t : t + 1])
+            nc.vector.scalar_tensor_tensor(res[:, t, :], s_win[t][:, :S], stat[:, t, 0:1], sg2[:, t, :], ALU.subtract, ALU.mult)
+            nc.sync.dma_start(out_rows[:, t, :], res[:, t, :])
+
+        res_bf = sb("res_bf", [P, S, PACK], BF16)
+        nc.vector.tensor_copy(res_bf[:].rearrange("p (c i) t -> p c t i", i=4), res[:].rearrange("p t (c i) -> p c t i", i=4))
+        o_w = sb("o_w", [P, S], U32)
+        o_s = sb("o_s", [P, S], U8)
+        nc.vector.quantize_mx(out=o_w[:].bitcast(FP8X4), scales=o_s[:], in_=res_bf[:].rearrange("p j t -> p (j t)"))
+        nc.sync.dma_start(out_1[0].rearrange("p n t -> p (n t)").bitcast(I32), o_w[:].bitcast(I32))
+        for q in range(4):
+            queue = nc.scalar if q % 2 == 0 else nc.sync
+            queue.dma_start(out_2[0, 4 * q : 4 * q + 4, :].bitcast(I32), o_s[32 * q : 32 * q + 4, :].bitcast(I32))

@@ -19,6 +19,7 @@ ACT = mybir.ActivationFunctionType
 P = 128
 PACK = 4
 WINDOW = 2 * S
+HALF = S // 2
 
 
 def tile_picked_twcmxbecn_none_po_kernel(tc, x_words, x_scales, w1_words, w1_scales, w2_words, w2_scales, sl, th, gs, sl2, offs, two, n1, n2, cand, n3, out_0, out_1, out_2):
@@ -58,25 +59,26 @@ def tile_picked_twcmxbecn_none_po_kernel(tc, x_words, x_scales, w1_words, w1_sca
         w1s_raw = sb("w1s_raw", [P, H], U8)
         nc.sync.dma_start(w2w_raw[:].bitcast(I32), w2_words[0].bitcast(I32))
         load_plane(nc.sync, w2s_raw, w2_scales)
-        n1_sb = load_list("n1_sb", n1)
         n2_sb = load_list("n2_sb", n2)
         nc.sync.dma_start(w1w_raw[:].bitcast(I32), w1_words[0].bitcast(I32))
+        sl_sb = load_rows(nc.sync, "sl_sb", sl)
+        th_sb = load_rows(nc.sync, "th_sb", th)
+        n1_sb = load_list("n1_sb", n1)
         load_plane(nc.sync, w1s_raw, w1_scales)
+        gs_sb = load_rows(nc.sync, "gs_sb", gs)
         n3_sb = load_list("n3_sb", n3)
-        sl_sb = load_rows(nc.gpsimd, "sl_sb", sl)
-        th_sb = load_rows(nc.gpsimd, "th_sb", th)
-        gs_sb = load_rows(nc.gpsimd, "gs_sb", gs)
-        sl2_sb = load_rows(nc.gpsimd, "sl2_sb", sl2)
+        sl2_sb = load_rows(nc.sync, "sl2_sb", sl2)
 
-        def gather(name, table, offsets, n, dtype, tag=""):
-            tile = sb(name, [P, n], dtype, tag)
-            nc.vector.tensor_copy(tile[:], table[:].indirect(offsets[:]))
-            return tile
+        warm_in = sb("warm_in", [P, 1], F32)
+        warm_out = sb("warm_out", [P, 1], F32)
+        nc.vector.memset(warm_in[:], 0.0)
+        nc.scalar.activation(warm_out[:], warm_in[:], ACT.Sigmoid)
 
-        def gather_dealt(name, table, offsets, n, dtype, tag=""):
-            tile = sb(name, [P, n], dtype, tag)
-            nc.vector.tensor_copy(tile[:].rearrange("p (t m) -> p m t", t=PACK), table[:].indirect(offsets[:]))
-            return tile
+        def gather(dst, table, offsets):
+            nc.vector.tensor_copy(dst, table[:].indirect(offsets[:]))
+
+        def dealt(ap):
+            return ap.rearrange("p (t m) -> p m t", t=PACK)
 
         def deal_words(name, raw):
             tile = sb(name, [P, 2 * H], U8)
@@ -88,99 +90,161 @@ def tile_picked_twcmxbecn_none_po_kernel(tc, x_words, x_scales, w1_words, w1_sca
             nc.vector.tensor_copy(tile[:].rearrange("p (t m) -> p t m", t=PACK), raw[:].rearrange("p (m t) -> p t m", t=PACK))
             return tile
 
-        two_s = gather("two_s", xs, two_sb, S, U8)
-        offs_s = gather("offs_s", xs, offs_sb, S, U8)
-        cand_s = gather_dealt("cand_s", xs, cand_sb, C, U8)
+        two_s = sb("two_s", [P, S], U8)
+        offs_s = sb("offs_s", [P, S], U8)
+        cand_s = sb("cand_s", [P, C], U8)
+        two_w = sb("two_w", [P, S], U32)
+        gather(two_s[:], xs, two_sb)
+        gather(offs_s[:], xs, offs_sb)
+        gather(dealt(cand_s[:]), xs, cand_sb)
         w2w = deal_words("w2w", w2w_raw)
-        two_w = gather("two_w", xw, two_sb, S, U32)
+        gather(two_w[:], xw, two_sb)
         w2s = deal_bytes("w2s", w2s_raw)
+        picked = sb("picked", [P, S + C], U32, "w2s_raw")
+        offs_w = picked[:, :S]
+        cand_w = picked[:, S:]
+        gather(offs_w, xw, offs_sb)
+        gather(dealt(cand_w), xw, cand_sb)
+        nb = sb("nb", [P, PACK], F32, "xw")
+        nc.vector.scalar_tensor_tensor(nb[:], sl_sb[:], -1.0, th_sb[:], ALU.mult, ALU.mult)
         w1w = deal_words("w1w", w1w_raw)
-        offs_w = gather("offs_w", xw, offs_sb, S, U32, "w2s_raw")
-
-        nb = sb("nb", [P, PACK], F32)
-        slth = sb("slth", [P, PACK], F32)
-        nc.gpsimd.tensor_tensor(slth[:], sl_sb[:], th_sb[:], ALU.mult)
-        nc.gpsimd.tensor_scalar(nb[:], slth[:], -1.0, 0.0, ALU.mult, ALU.add)
+        w1s = deal_bytes("w1s", w1s_raw)
 
         def weight_product(bank, words, scales, t, xw_g, xs_g):
             nc.tensor.matmul_mx(
-                out=bank[:],
+                out=bank,
                 lhsT=words[:, 2 * P * t : 2 * P * (t + 1)].bitcast(FP4X4),
                 lhsT_scale=scales[:, P * t : P * (t + 1)],
-                rhs=xw_g[:].bitcast(FP8X4),
+                rhs=xw_g.bitcast(FP8X4),
                 rhs_scale=xs_g[:],
                 start=True,
                 stop=True,
             )
 
         d_ps = [psum.tile([P, S], F32, name=f"d_ps{t}", tag=f"first{t}") for t in range(PACK)]
-        y_ps = [psum.tile([P, S], F32, name=f"y_ps{t}") for t in range(PACK)]
+        y_ps = [psum.tile([P, 2, S], F32, name=f"y_ps{u}") for u in range(2)]
         for t in range(PACK):
-            weight_product(d_ps[t], w2w, w2s, t, two_w, two_s)
-        w1s = deal_bytes("w1s", w1s_raw)
+            weight_product(d_ps[t][:], w2w, w2s, t, two_w[:], two_s)
         for t in range(PACK):
-            weight_product(y_ps[t], w1w, w1s, t, offs_w, offs_s)
+            weight_product(y_ps[t // 2][:, t % 2, :], w1w, w1s, t, offs_w, offs_s)
 
-        cand_w = gather_dealt("cand_w", xw, cand_sb, C, U32, "w1s_raw")
+        def pieces(t):
+            return [(0, 2)] if t < PACK - 1 else [(0, 1), (1, 2)]
+
+        def by_half(ap):
+            return ap.rearrange("p (h j) -> p h j", j=HALF)
+
+        def interleaved(dst, src):
+            return dst.rearrange("p (c i) t -> p c t i", i=4), src.rearrange("p t (c i) -> p c t i", i=4)
 
         d_win = [sb(f"d_win{t}", [P, WINDOW], F32) for t in range(PACK)]
         sg = sb("sg", [P, PACK, S], F32)
         dn2 = sb("dn2", [P, PACK, S], F32)
         ysg = sb("ysg", [P, PACK, S], F32)
-        diff = sb("diff", [P, PACK, S], F32)
-        larger = sb("larger", [P, PACK, S], F32)
-        for t in range(PACK):
-            nc.scalar.copy(d_win[t][:, :S], d_ps[t][:])
-            nc.scalar.activation(sg[:, t, :], d_win[t][:].indirect(n1_sb[:]), ACT.Sigmoid, bias=nb[:, t : t + 1], scale=sl_sb[:, t : t + 1])
-            nc.scalar.activation(dn2[:, t, :], d_win[t][:].indirect(n2_sb[:]), ACT.Copy)
-            nc.vector.tensor_tensor(ysg[:, t, :], y_ps[t][:], sg[:, t, :], ALU.mult)
-            nc.vector.tensor_tensor(diff[:, t, :], dn2[:, t, :], d_win[t][:, :S], ALU.subtract)
-            nc.vector.tensor_tensor(larger[:, t, :], ysg[:, t, :], diff[:, t, :], ALU.max)
-
+        diff = sb("diff", [P, PACK, S], F32, "w1s_raw")
+        larger = sb("larger", [P, 2, PACK, HALF], F32)
         z_bf = sb("z_bf", [P, S, PACK], BF16)
-        nc.vector.tensor_tensor(
-            z_bf[:].rearrange("p (c i) t -> p c t i", i=4),
-            larger[:].rearrange("p t (c i) -> p c t i", i=4),
-            gs_sb[:].unsqueeze(1).unsqueeze(3).to_broadcast([P, S // 4, PACK, 4]),
-            ALU.mult,
-        )
         z_w = sb("z_w", [P, S], U32)
         z_s = sb("z_s", [P, S], U8)
-        nc.vector.quantize_mx(out=z_w[:].bitcast(FP8X4), scales=z_s[:], in_=z_bf[:].rearrange("p j t -> p (j t)"))
 
-        coef = sb("coef", [P, 2, PACK], F32)
-        nc.gpsimd.memset(coef[:, 0, :], 1.0 / S)
-        nc.gpsimd.tensor_scalar(coef[:, 1, :], sl2_sb[:], -1.0 / S, 0.0, ALU.mult, ALU.add)
+        def fetch_n2(t):
+            nc.scalar.activation(dn2[:, t, :], d_win[t][:].indirect(n2_sb[:]), ACT.Copy)
+
+        def fetch_gate(t):
+            nc.scalar.activation(sg[:, t, :], d_win[t][:].indirect(n1_sb[:]), ACT.Sigmoid, bias=nb[:, t : t + 1], scale=sl_sb[:, t : t + 1])
+
+        def difference(t):
+            nc.vector.tensor_tensor(diff[:, t, :], dn2[:, t, :], d_win[t][:, :S], ALU.subtract)
+
+        def gated(t0, t1):
+            nc.vector.tensor_tensor(ysg[:, t0:t1, :], y_ps[t0 // 2][:, t0 % 2 : t0 % 2 + t1 - t0, :], sg[:, t0:t1, :], ALU.mult)
+
+        def take_larger(t0, t1, h0, h1):
+            view = lambda tile: tile[:, t0:t1, h0 * HALF : h1 * HALF].rearrange("p t (h j) -> p h t j", j=HALF)
+            nc.vector.tensor_tensor(larger[:, h0:h1, t0:t1, :], view(ysg), view(diff), ALU.max)
+
+        for t in (0, 1):
+            nc.scalar.copy(d_win[t][:, :S], d_ps[t][:])
+            fetch_n2(t)
+        for t in (2, 3):
+            nc.vector.tensor_copy(d_win[t][:, :S], d_ps[t][:])
+        for t in (0, 1):
+            fetch_gate(t)
+            difference(t)
+        for t in (2, 3):
+            fetch_n2(t)
+        for t in (2, 3):
+            fetch_gate(t)
+        gated(0, 2)
+        difference(2)
+        take_larger(0, 2, 0, 2)
+        difference(3)
+        gated(2, 3)
+        take_larger(2, 3, 0, 2)
+        gated(3, 4)
+        for h in range(2):
+            take_larger(3, 4, h, h + 1)
+
+        halves = [slice(h * HALF, (h + 1) * HALF) for h in range(2)]
+        s_ps = [psum.tile([P, S], F32, name=f"s_ps{t}", tag=f"first{t}") for t in range(PACK)]
+        for h, cols in enumerate(halves):
+            dst, src = interleaved(z_bf[:, cols, :], larger[:, h, :, :])
+            nc.vector.tensor_tensor(dst, src, gs_sb[:].unsqueeze(1).unsqueeze(3).to_broadcast([P, HALF // 4, PACK, 4]), ALU.mult)
+        for cols in halves:
+            nc.vector.quantize_mx(out=z_w[:, cols].bitcast(FP8X4), scales=z_s[:, cols], in_=z_bf[:, cols, :].rearrange("p j t -> p (j t)"))
+        for cols in halves:
+            for t in range(PACK):
+                nc.tensor.matmul_mx(
+                    out=s_ps[t][:, cols],
+                    lhsT=cand_w[:, P * t : P * (t + 1)].bitcast(FP8X4),
+                    lhsT_scale=cand_s[:, P * t : P * (t + 1)],
+                    rhs=z_w[:, cols].bitcast(FP8X4),
+                    rhs_scale=z_s[:, cols],
+                    start=True,
+                    stop=True,
+                )
 
         s_win = [sb(f"s_win{t}", [P, WINDOW], F32) for t in range(PACK)]
         total = sb("total", [P, PACK], F32)
-        stat = sb("stat", [P, PACK, 2], F32)
+        mu = sb("mu", [P, PACK], F32)
+        nb2 = sb("nb2", [P, PACK], F32)
         sg2 = sb("sg2", [P, PACK, S], F32)
-        res = sb("res", [P, PACK, S], F32)
-        out_rows = out_0.rearrange("(p t) j -> p t j", t=PACK)
+        res = sb("res", [P, 2, PACK, HALF], F32)
+        out_rows = out_0.rearrange("(p t) (h j) -> p h t j", t=PACK, j=HALF)
+
+        def scores(t):
+            nc.vector.tensor_scalar(s_win[t][:, :S], s_ps[t][:], 0.0625, None, ALU.mult, ALU.add, accum_out=total[:, t : t + 1])
+
+        def bias_pair(pair):
+            nc.vector.scalar_tensor_tensor(nb2[:, pair], total[:, pair], -1.0 / S, sl2_sb[:, pair], ALU.mult, ALU.mult)
+
+        def mean_pair(pair):
+            nc.vector.tensor_scalar(mu[:, pair], total[:, pair], 1.0 / S, None, ALU.mult)
+
+        nc.scalar.activation(s_win[0][:, :S], s_ps[0][:], ACT.Copy, scale=0.0625, accum_out=total[:, 0:1])
+        scores(1)
+        bias_pair(slice(0, 2))
+        scores(2)
+        mean_pair(slice(0, 2))
+        scores(3)
+        bias_pair(slice(2, 4))
+        mean_pair(slice(2, 4))
         for t in range(PACK):
-            s_ps = psum.tile([P, S], F32, name=f"s_ps{t}", tag=f"first{t}")
-            nc.tensor.matmul_mx(
-                out=s_ps[:],
-                lhsT=cand_w[:, P * t : P * (t + 1)].bitcast(FP8X4),
-                lhsT_scale=cand_s[:, P * t : P * (t + 1)],
-                rhs=z_w[:].bitcast(FP8X4),
-                rhs_scale=z_s[:],
-                start=True,
-                stop=True,
-            )
-            nc.vector.tensor_scalar(s_win[t][:, :S], s_ps[:], 0.0625, None, ALU.mult, ALU.add, accum_out=total[:, t : t + 1])
-            nc.vector.tensor_scalar(stat[:, t, :], coef[:, :, t], total[:, t : t + 1], None, ALU.mult)
-        for t in range(PACK):
-            nc.scalar.activation(sg2[:, t, :], s_win[t][:].indirect(n3_sb[:]), ACT.Sigmoid, bias=stat[:, t, 1:2], scale=sl2_sb[:, t : t + 1])
-            nc.vector.scalar_tensor_tensor(res[:, t, :], s_win[t][:, :S], stat[:, t, 0:1], sg2[:, t, :], ALU.subtract, ALU.mult)
-            nc.sync.dma_start(out_rows[:, t, :], res[:, t, :])
+            col = slice(t, t + 1)
+            nc.scalar.activation(sg2[:, t, :], s_win[t][:].indirect(n3_sb[:]), ACT.Sigmoid, bias=nb2[:, col], scale=sl2_sb[:, col])
+            for h0, h1 in pieces(t):
+                cols = slice(h0 * HALF, h1 * HALF)
+                nc.vector.scalar_tensor_tensor(res[:, h0:h1, t, :], by_half(s_win[t][:, cols]), mu[:, col], by_half(sg2[:, t, cols]), ALU.subtract, ALU.mult)
+            nc.sync.dma_start(out_rows[:, :, t, :], res[:, :, t, :])
 
         res_bf = sb("res_bf", [P, S, PACK], BF16)
-        nc.vector.tensor_copy(res_bf[:].rearrange("p (c i) t -> p c t i", i=4), res[:].rearrange("p t (c i) -> p c t i", i=4))
         o_w = sb("o_w", [P, S], U32)
         o_s = sb("o_s", [P, S], U8)
-        nc.vector.quantize_mx(out=o_w[:].bitcast(FP8X4), scales=o_s[:], in_=res_bf[:].rearrange("p j t -> p (j t)"))
+        for h, cols in enumerate(halves):
+            dst, src = interleaved(res_bf[:, cols, :], res[:, h, :, :])
+            nc.vector.tensor_copy(dst, src)
+        for cols in halves:
+            nc.vector.quantize_mx(out=o_w[:, cols].bitcast(FP8X4), scales=o_s[:, cols], in_=res_bf[:, cols, :].rearrange("p j t -> p (j t)"))
         nc.sync.dma_start(out_1[0].rearrange("p n t -> p (n t)").bitcast(I32), o_w[:].bitcast(I32))
         for q in range(4):
             queue = nc.scalar if q % 2 == 0 else nc.sync

@@ -142,7 +142,8 @@ def tile_picked_twcmxbecn_none_po_kernel(tc, x_words, x_scales, w1_words, w1_sca
         dn2 = sb("dn2", [P, PACK, S], F32)
         ysg = sb("ysg", [P, PACK, S], F32)
         diff = sb("diff", [P, PACK, S], F32, "w1s_raw")
-        larger = sb("larger", [P, 2, PACK, HALF], F32)
+        larger = sb("larger", [P, PACK, S], F32)
+        z_rows = sb("z_rows", [P, 2, PACK, HALF], BF16)
         z_bf = sb("z_bf", [P, S, PACK], BF16)
         z_w = sb("z_w", [P, S], U32)
         z_s = sb("z_s", [P, S], U8)
@@ -159,51 +160,56 @@ def tile_picked_twcmxbecn_none_po_kernel(tc, x_words, x_scales, w1_words, w1_sca
         def gated(t0, t1):
             nc.vector.tensor_tensor(ysg[:, t0:t1, :], y_ps[t0 // 2][:, t0 % 2 : t0 % 2 + t1 - t0, :], sg[:, t0:t1, :], ALU.mult)
 
-        def take_larger(t0, t1, h0, h1):
-            view = lambda tile: tile[:, t0:t1, h0 * HALF : h1 * HALF].rearrange("p t (h j) -> p h t j", j=HALF)
-            nc.vector.tensor_tensor(larger[:, h0:h1, t0:t1, :], view(ysg), view(diff), ALU.max)
+        def take_larger(t0, t1, cols):
+            nc.vector.tensor_tensor(larger[:, t0:t1, cols], ysg[:, t0:t1, cols], diff[:, t0:t1, cols], ALU.max)
 
+        halves = [slice(h * HALF, (h + 1) * HALF) for h in range(2)]
         for t in (0, 1):
             nc.scalar.copy(d_win[t][:, :S], d_ps[t][:])
             fetch_n2(t)
-        for t in (2, 3):
-            nc.vector.tensor_copy(d_win[t][:, :S], d_ps[t][:])
-        for t in (0, 1):
-            fetch_gate(t)
-            difference(t)
-        for t in (2, 3):
-            fetch_n2(t)
-        for t in (2, 3):
-            fetch_gate(t)
+        nc.scalar.copy(d_win[2][:, :S], d_ps[2][:])
+        fetch_gate(0)
+        fetch_gate(1)
+        fetch_n2(2)
+        fetch_gate(2)
+        nc.vector.tensor_copy(d_win[3][:, :S], d_ps[3][:])
+        fetch_gate(3)
+        difference(0)
+        nc.vector.tensor_copy(dn2[:, 3, :], d_win[3][:].indirect(n2_sb[:]))
+        difference(1)
+        difference(3)
         gated(0, 2)
         difference(2)
-        take_larger(0, 2, 0, 2)
-        difference(3)
+        take_larger(0, 2, slice(0, S))
         gated(2, 3)
-        take_larger(2, 3, 0, 2)
+        take_larger(2, 3, slice(0, S))
         gated(3, 4)
-        for h in range(2):
-            take_larger(3, 4, h, h + 1)
+        for cols in halves:
+            take_larger(3, 4, cols)
+        for t in range(PACK - 1):
+            nc.scalar.activation(z_rows[:, :, t, :], by_half(larger[:, t, :]), ACT.Copy, scale=gs_sb[:, t : t + 1])
+        for h, cols in enumerate(halves):
+            nc.vector.tensor_scalar(z_rows[:, h, 3, :], larger[:, 3, cols], gs_sb[:, 3:4], None, ALU.mult)
 
-        halves = [slice(h * HALF, (h + 1) * HALF) for h in range(2)]
         s_ps = [psum.tile([P, S], F32, name=f"s_ps{t}", tag=f"first{t}") for t in range(PACK)]
         for h, cols in enumerate(halves):
-            dst, src = interleaved(z_bf[:, cols, :], larger[:, h, :, :])
-            nc.vector.tensor_tensor(dst, src, gs_sb[:].unsqueeze(1).unsqueeze(3).to_broadcast([P, HALF // 4, PACK, 4]), ALU.mult)
+            dst, src = interleaved(z_bf[:, cols, :], z_rows[:, h, :, :])
+            nc.vector.tensor_copy(dst, src)
         for cols in halves:
             nc.vector.quantize_mx(out=z_w[:, cols].bitcast(FP8X4), scales=z_s[:, cols], in_=z_bf[:, cols, :].rearrange("p j t -> p (j t)"))
-        for cols in halves:
-            for t in range(PACK):
-                nc.tensor.matmul_mx(
-                    out=s_ps[t][:, cols],
-                    lhsT=cand_w[:, P * t : P * (t + 1)].bitcast(FP8X4),
-                    lhsT_scale=cand_s[:, P * t : P * (t + 1)],
-                    rhs=z_w[:, cols].bitcast(FP8X4),
-                    rhs_scale=z_s[:, cols],
-                    start=True,
-                    stop=True,
-                )
+        for t in range(PACK):
+            nc.tensor.matmul_mx(
+                out=s_ps[t][:],
+                lhsT=cand_w[:, P * t : P * (t + 1)].bitcast(FP8X4),
+                lhsT_scale=cand_s[:, P * t : P * (t + 1)],
+                rhs=z_w[:].bitcast(FP8X4),
+                rhs_scale=z_s[:],
+                start=True,
+                stop=True,
+            )
 
+        slope0 = sb("slope0", [P, 1], F32)
+        nc.scalar.activation(slope0[:], sl2_sb[:, 0:1], ACT.Copy, scale=-1.0 / S)
         s_win = [sb(f"s_win{t}", [P, WINDOW], F32) for t in range(PACK)]
         total = sb("total", [P, PACK], F32)
         mu = sb("mu", [P, PACK], F32)
@@ -222,8 +228,9 @@ def tile_picked_twcmxbecn_none_po_kernel(tc, x_words, x_scales, w1_words, w1_sca
             nc.vector.tensor_scalar(mu[:, pair], total[:, pair], 1.0 / S, None, ALU.mult)
 
         nc.scalar.activation(s_win[0][:, :S], s_ps[0][:], ACT.Copy, scale=0.0625, accum_out=total[:, 0:1])
+        nc.scalar.activation(nb2[:, 0:1], total[:, 0:1], ACT.Copy, scale=slope0[:])
         scores(1)
-        bias_pair(slice(0, 2))
+        bias_pair(slice(1, 2))
         scores(2)
         mean_pair(slice(0, 2))
         scores(3)
@@ -231,9 +238,10 @@ def tile_picked_twcmxbecn_none_po_kernel(tc, x_words, x_scales, w1_words, w1_sca
         mean_pair(slice(2, 4))
         for t in range(PACK):
             col = slice(t, t + 1)
-            nc.scalar.activation(sg2[:, t, :], s_win[t][:].indirect(n3_sb[:]), ACT.Sigmoid, bias=nb2[:, col], scale=sl2_sb[:, col])
             for h0, h1 in pieces(t):
                 cols = slice(h0 * HALF, h1 * HALF)
+                ent = slice(h0 * HALF // 16, h1 * HALF // 16)
+                nc.scalar.activation(sg2[:, t, cols], s_win[t][:].indirect(n3_sb[:, ent]), ACT.Sigmoid, bias=nb2[:, col], scale=sl2_sb[:, col])
                 nc.vector.scalar_tensor_tensor(res[:, h0:h1, t, :], by_half(s_win[t][:, cols]), mu[:, col], by_half(sg2[:, t, cols]), ALU.subtract, ALU.mult)
             nc.sync.dma_start(out_rows[:, :, t, :], res[:, :, t, :])
 

from contextlib import ExitStack

import concourse.mybir as mybir

K, T, S, H, C = 512, 2048, 256, 512, 512
FLOPS = 2 * K * S * (H + H + C)

F32 = mybir.dt.float32
BF16 = mybir.dt.bfloat16
I32 = mybir.dt.int32
U32 = mybir.dt.uint32
U16 = mybir.dt.uint16
U8 = mybir.dt.uint8
FP8X4 = mybir.dt.float8_e4m3fn_x4
FP4X4 = mybir.dt.float4_e2m1fn_x4
ALU = mybir.AluOpType
ACT = mybir.ActivationFunctionType

P = 128
PACK = 4
WINDOW = 2 * S
HALF = S // 2


def tile_picked_twcmxbecn_none_po_kernel(tc, x_words, x_scales, w1_words, w1_scales, w2_words, w2_scales, sl, th, gs, sl2, offs, two, n1, n2, cand, n3, out_0, out_1, out_2):
    nc = tc.nc
    with ExitStack() as ctx:
        keep = ctx.enter_context(tc.tile_pool(name="keep", bufs=1))
        psum = ctx.enter_context(tc.psum_pool(name="psum", bufs=1))

        def sb(name, shape, dtype, tag=""):
            return keep.tile(shape, dtype, name=name, tag=tag or name, align_bytes=64)

        def load_list(name, src):
            tile = sb(name, list(src.shape), U16)
            nc.sync.dma_start(tile[:], src)
            return tile

        def load_plane(queue, tile, src):
            words = src.shape[2] // 4
            for q in range(4):
                queue.dma_start(tile[32 * q : 32 * q + 32, :].bitcast(I32), src[0, 4 * q : 4 * q + 4, :].bitcast(I32).unsqueeze(0).to_broadcast([8, 4, words]))

        def load_rows(queue, name, src):
            tile = sb(name, [P, PACK], F32)
            queue.dma_start(tile[:], src.rearrange("(p t) o -> p (t o)", t=PACK))
            return tile

        xs = sb("xs", [P, T], U8)
        load_plane(nc.sync, xs, x_scales)
        two_sb = load_list("two_sb", two)
        offs_sb = load_list("offs_sb", offs)
        cand_sb = load_list("cand_sb", cand)
        xw = sb("xw", [P, T], U32)
        nc.sync.dma_start(xw[:].bitcast(I32), x_words[0].rearrange("p n t -> p (n t)").bitcast(I32))
        w2w_raw = sb("w2w_raw", [P, 2 * H], U8)
        w1w_raw = sb("w1w_raw", [P, 2 * H], U8)
        w2s_raw = sb("w2s_raw", [P, H], U8)
        w1s_raw = sb("w1s_raw", [P, H], U8)
        nc.sync.dma_start(w2w_raw[:].bitcast(I32), w2_words[0].bitcast(I32))
        load_plane(nc.sync, w2s_raw, w2_scales)
        n2_sb = load_list("n2_sb", n2)
        nc.sync.dma_start(w1w_raw[:].bitcast(I32), w1_words[0].bitcast(I32))
        sl_sb = load_rows(nc.sync, "sl_sb", sl)
        th_sb = load_rows(nc.sync, "th_sb", th)
        n1_sb = load_list("n1_sb", n1)
        load_plane(nc.sync, w1s_raw, w1_scales)
        gs_sb = load_rows(nc.sync, "gs_sb", gs)
        n3_sb = load_list("n3_sb", n3)
        sl2_sb = load_rows(nc.sync, "sl2_sb", sl2)

        warm_in = sb("warm_in", [P, 1], F32)
        warm_out = sb("warm_out", [P, 1], F32)
        nc.vector.memset(warm_in[:], 0.0)
        nc.scalar.activation(warm_out[:], warm_in[:], ACT.Sigmoid)

        def gather(dst, table, offsets):
            nc.vector.tensor_copy(dst, table[:].indirect(offsets[:]))

        def dealt(ap):
            return ap.rearrange("p (t m) -> p m t", t=PACK)

        def deal_words(name, raw):
            tile = sb(name, [P, 2 * H], U8)
            nc.scalar.copy(tile[:].bitcast(U16).rearrange("p (t m) -> p t m", t=PACK), raw[:].bitcast(U16).rearrange("p (m t) -> p t m", t=PACK))
            return tile

        def deal_bytes(name, raw):
            tile = sb(name, [P, H], U8)
            nc.vector.tensor_copy(tile[:].rearrange("p (t m) -> p t m", t=PACK), raw[:].rearrange("p (m t) -> p t m", t=PACK))
            return tile

        two_s = sb("two_s", [P, S], U8)
        offs_s = sb("offs_s", [P, S], U8)
        cand_s = sb("cand_s", [P, C], U8)
        two_w = sb("two_w", [P, S], U32)
        gather(two_s[:], xs, two_sb)
        gather(offs_s[:], xs, offs_sb)
        gather(dealt(cand_s[:]), xs, cand_sb)
        w2w = deal_words("w2w", w2w_raw)
        gather(two_w[:], xw, two_sb)
        w2s = deal_bytes("w2s", w2s_raw)
        picked = sb("picked", [P, S + C], U32, "w2s_raw")
        offs_w = picked[:, :S]
        cand_w = picked[:, S:]
        gather(offs_w, xw, offs_sb)
        gather(dealt(cand_w), xw, cand_sb)
        nb = sb("nb", [P, PACK], F32, "xw")
        nc.vector.scalar_tensor_tensor(nb[:], sl_sb[:], -1.0, th_sb[:], ALU.mult, ALU.mult)
        w1w = deal_words("w1w", w1w_raw)
        w1s = deal_bytes("w1s", w1s_raw)

        def weight_product(bank, words, scales, t, xw_g, xs_g):
            nc.tensor.matmul_mx(
                out=bank,
                lhsT=words[:, 2 * P * t : 2 * P * (t + 1)].bitcast(FP4X4),
                lhsT_scale=scales[:, P * t : P * (t + 1)],
                rhs=xw_g.bitcast(FP8X4),
                rhs_scale=xs_g[:],
                start=True,
                stop=True,
            )

        d_ps = [psum.tile([P, S], F32, name=f"d_ps{t}", tag=f"first{t}") for t in range(PACK)]
        y_ps = [psum.tile([P, 2, S], F32, name=f"y_ps{u}") for u in range(2)]
        for t in range(PACK):
            weight_product(d_ps[t][:], w2w, w2s, t, two_w[:], two_s)
        for t in range(PACK):
            weight_product(y_ps[t // 2][:, t % 2, :], w1w, w1s, t, offs_w, offs_s)

        def pieces(t):
            return [(0, 2)] if t < PACK - 1 else [(0, 1), (1, 2)]

        def by_half(ap):
            return ap.rearrange("p (h j) -> p h j", j=HALF)

        def interleaved(dst, src):
            return dst.rearrange("p (c i) t -> p c t i", i=4), src.rearrange("p t (c i) -> p c t i", i=4)

        d_win = [sb(f"d_win{t}", [P, WINDOW], F32) for t in range(PACK)]
        sg = sb("sg", [P, PACK, S], F32)
        dn2 = sb("dn2", [P, PACK, S], F32)
        ysg = sb("ysg", [P, PACK, S], F32)
        diff = sb("diff", [P, PACK, S], F32, "w1s_raw")
        larger = sb("larger", [P, PACK, S], F32)
        z_rows = sb("z_rows", [P, 2, PACK, HALF], BF16)
        z_bf = sb("z_bf", [P, S, PACK], BF16)
        z_w = sb("z_w", [P, S], U32)
        z_s = sb("z_s", [P, S], U8)

        def fetch_n2(t):
            nc.scalar.activation(dn2[:, t, :], d_win[t][:].indirect(n2_sb[:]), ACT.Copy)

        def fetch_gate(t):
            nc.scalar.activation(sg[:, t, :], d_win[t][:].indirect(n1_sb[:]), ACT.Sigmoid, bias=nb[:, t : t + 1], scale=sl_sb[:, t : t + 1])

        def difference(t):
            nc.vector.tensor_tensor(diff[:, t, :], dn2[:, t, :], d_win[t][:, :S], ALU.subtract)

        def gated(t0, t1):
            nc.vector.tensor_tensor(ysg[:, t0:t1, :], y_ps[t0 // 2][:, t0 % 2 : t0 % 2 + t1 - t0, :], sg[:, t0:t1, :], ALU.mult)

        def take_larger(t0, t1, cols):
            nc.vector.tensor_tensor(larger[:, t0:t1, cols], ysg[:, t0:t1, cols], diff[:, t0:t1, cols], ALU.max)

        halves = [slice(h * HALF, (h + 1) * HALF) for h in range(2)]
        for t in (0, 1):
            nc.scalar.copy(d_win[t][:, :S], d_ps[t][:])
            fetch_n2(t)
        nc.scalar.copy(d_win[2][:, :S], d_ps[2][:])
        fetch_gate(0)
        fetch_gate(1)
        fetch_n2(2)
        fetch_gate(2)
        nc.vector.tensor_copy(d_win[3][:, :S], d_ps[3][:])
        fetch_gate(3)
        difference(0)
        nc.vector.tensor_copy(dn2[:, 3, :], d_win[3][:].indirect(n2_sb[:]))
        difference(1)
        difference(3)
        gated(0, 2)
        difference(2)
        take_larger(0, 2, slice(0, S))
        gated(2, 3)
        take_larger(2, 3, slice(0, S))
        gated(3, 4)
        for cols in halves:
            take_larger(3, 4, cols)
        for t in range(PACK - 1):
            nc.scalar.activation(z_rows[:, :, t, :], by_half(larger[:, t, :]), ACT.Copy, scale=gs_sb[:, t : t + 1])
        for h, cols in enumerate(halves):
            nc.vector.tensor_scalar(z_rows[:, h, 3, :], larger[:, 3, cols], gs_sb[:, 3:4], None, ALU.mult)

        s_ps = [psum.tile([P, S], F32, name=f"s_ps{t}", tag=f"first{t}") for t in range(PACK)]
        for h, cols in enumerate(halves):
            dst, src = interleaved(z_bf[:, cols, :], z_rows[:, h, :, :])
            nc.vector.tensor_copy(dst, src)
        for cols in halves:
            nc.vector.quantize_mx(out=z_w[:, cols].bitcast(FP8X4), scales=z_s[:, cols], in_=z_bf[:, cols, :].rearrange("p j t -> p (j t)"))
        for t in range(PACK):
            nc.tensor.matmul_mx(
                out=s_ps[t][:],
                lhsT=cand_w[:, P * t : P * (t + 1)].bitcast(FP8X4),
                lhsT_scale=cand_s[:, P * t : P * (t + 1)],
                rhs=z_w[:].bitcast(FP8X4),
                rhs_scale=z_s[:],
                start=True,
                stop=True,
            )

        slope0 = sb("slope0", [P, 1], F32)
        nc.scalar.activation(slope0[:], sl2_sb[:, 0:1], ACT.Copy, scale=-1.0 / S)
        s_win = [sb(f"s_win{t}", [P, WINDOW], F32) for t in range(PACK)]
        total = sb("total", [P, PACK], F32)
        mu = sb("mu", [P, PACK], F32)
        nb2 = sb("nb2", [P, PACK], F32)
        sg2 = sb("sg2", [P, PACK, S], F32)
        res = sb("res", [P, 2, PACK, HALF], F32)
        out_rows = out_0.rearrange("(p t) (h j) -> p h t j", t=PACK, j=HALF)

        def scores(t):
            nc.vector.tensor_scalar(s_win[t][:, :S], s_ps[t][:], 0.0625, None, ALU.mult, ALU.add, accum_out=total[:, t : t + 1])

        def bias_pair(pair):
            nc.vector.scalar_tensor_tensor(nb2[:, pair], total[:, pair], -1.0 / S, sl2_sb[:, pair], ALU.mult, ALU.mult)

        def mean_pair(pair):
            nc.vector.tensor_scalar(mu[:, pair], total[:, pair], 1.0 / S, None, ALU.mult)

        nc.scalar.activation(s_win[0][:, :S], s_ps[0][:], ACT.Copy, scale=0.0625, accum_out=total[:, 0:1])
        nc.scalar.activation(nb2[:, 0:1], total[:, 0:1], ACT.Copy, scale=slope0[:])
        scores(1)
        bias_pair(slice(1, 2))
        scores(2)
        mean_pair(slice(0, 2))
        scores(3)
        bias_pair(slice(2, 4))
        mean_pair(slice(2, 4))
        for t in range(PACK):
            col = slice(t, t + 1)
            for h0, h1 in pieces(t):
                cols = slice(h0 * HALF, h1 * HALF)
                ent = slice(h0 * HALF // 16, h1 * HALF // 16)
                nc.scalar.activation(sg2[:, t, cols], s_win[t][:].indirect(n3_sb[:, ent]), ACT.Sigmoid, bias=nb2[:, col], scale=sl2_sb[:, col])
                nc.vector.scalar_tensor_tensor(res[:, h0:h1, t, :], by_half(s_win[t][:, cols]), mu[:, col], by_half(sg2[:, t, cols]), ALU.subtract, ALU.mult)
            nc.sync.dma_start(out_rows[:, :, t, :], res[:, :, t, :])

        res_bf = sb("res_bf", [P, S, PACK], BF16)
        o_w = sb("o_w", [P, S], U32)
        o_s = sb("o_s", [P, S], U8)
        for h, cols in enumerate(halves):
            dst, src = interleaved(res_bf[:, cols, :], res[:, h, :, :])
            nc.vector.tensor_copy(dst, src)
        for cols in halves:
            nc.vector.quantize_mx(out=o_w[:, cols].bitcast(FP8X4), scales=o_s[:, cols], in_=res_bf[:, cols, :].rearrange("p j t -> p (j t)"))
        nc.sync.dma_start(out_1[0].rearrange("p n t -> p (n t)").bitcast(I32), o_w[:].bitcast(I32))
        for q in range(4):
            queue = nc.scalar if q % 2 == 0 else nc.sync
            queue.dma_start(out_2[0, 4 * q : 4 * q + 4, :].bitcast(I32), o_s[32 * q : 32 * q + 4, :].bitcast(I32))
